import numpy as np
import ml_dtypes


def mxq(x, axis, fmt="e4m3"):
    dtype, down = {"e4m3": (ml_dtypes.float8_e4m3fn, 7), "e5m2": (ml_dtypes.float8_e5m2, 14)}[fmt]
    v = np.moveaxis(np.asarray(x, np.float32).astype(ml_dtypes.bfloat16).astype(np.float64), axis, -1)
    blocks = v.reshape(v.shape[:-1] + (-1, 32))
    amax = np.abs(blocks).max(-1, keepdims=True)
    byte = np.maximum(np.where(amax > 0, np.frexp(amax)[1] - 1 + 127, 0) - down, 1)
    scale = np.exp2(byte - 127.0)
    codes = (blocks / scale).astype(np.float32).astype(dtype).astype(np.float64)
    return np.moveaxis((codes * scale).reshape(v.shape), -1, axis)


WIDE = False


def mx_kscale(k):
    if not WIDE:
        return np.ones(k)
    levels = np.array([10, -10, 5, -5, 0])
    if k % 512:
        return np.exp2(np.random.permutation(np.resize(levels, k // 32))).repeat(32)
    a = np.empty((k // 512, 16))
    for p in range(k // 512):
        a[p, :8] = np.random.permutation(np.resize(levels, 8))
        for g in range(8):
            far = levels[np.abs(levels - a[p, g]) >= 10]
            a[p, g + 8] = far[np.random.randint(len(far))]
    return np.exp2(a.ravel()).repeat(32)


def f64(x):
    return np.asarray(x).astype(np.float64)


def striped(idx):
    return np.tile(idx.reshape(-1, 16).T, (8, 1)).astype(np.uint16)


def unstriped(offs):
    return offs[:16].T.reshape(-1).astype(np.int64)


E2M1 = np.array([0.0, 0.5, 1.0, 1.5, 2.0, 3.0, 4.0, 6.0, -0.0, -0.5, -1.0, -1.5, -2.0, -3.0, -4.0, -6.0])


def pack_weight(w, fmt):
    k, n = w.shape
    w = f64(np.asarray(w, np.float32).astype(ml_dtypes.bfloat16)).reshape(k // 32, 32, n)
    amax = np.abs(w).max(1)
    if fmt == "e4m3":
        byte = np.frexp(amax)[1] - 1 + 127 - 7
    else:
        mant, ex = np.frexp(amax / 6.0)
        byte = np.where(mant > 0.5, ex, ex - 1) + 127
    byte = np.clip(np.where(amax > 0, byte, 1), 1, 254)
    scaled = (w * np.exp2(127.0 - byte)[:, None, :]).reshape(k, n).astype(np.float32)
    by_word = np.ascontiguousarray(scaled.reshape(k // 512, 128, 4, n).transpose(0, 1, 3, 2))
    if fmt == "e4m3":
        words = by_word.astype(ml_dtypes.float8_e4m3fn).view(np.uint8)
    else:
        c = by_word.astype(ml_dtypes.float4_e2m1fn).view(np.uint8) & 0xF
        words = (c[..., 0::2] | (c[..., 1::2] << 4)).reshape(k // 512, 128, 2 * n)
    return np.ascontiguousarray(words), np.ascontiguousarray(byte.astype(np.uint8).reshape(k // 512, 16, n))


def unpack_weight(words, scales, fmt):
    g, _, n = scales.shape
    words = np.ascontiguousarray(words).reshape(g, 128, n, -1)
    if fmt == "e4m3":
        vals = words.view(ml_dtypes.float8_e4m3fn).astype(np.float64)
    else:
        nib = np.empty((g, 128, n, 4), np.uint8)
        nib[..., 0::2] = words & 0xF
        nib[..., 1::2] = words >> 4
        vals = E2M1[nib]
    vals = vals * np.repeat(np.exp2(scales.astype(np.float64) - 127.0), 8, axis=1)[..., None]
    return vals.transpose(0, 1, 3, 2).reshape(g * 512, n)


def gelu(v):
    return 0.5 * v * (1.0 + np.tanh(np.sqrt(2.0 / np.pi) * (v + 0.044715 * v**3)))


K, T, S, H, P = 1536, 4096, 1024, 1024, 512

def setup_inputs():
    n = np.random.standard_normal
    s = mx_kscale(K)[:, None]
    u = mx_kscale(H)[:, None]
    tab_words, tab_scales = pack_weight(n((K, T)) * s, "e4m3")
    w4_words, w4_scales = pack_weight(1.3 * n((H, H)) / np.sqrt(H) / u, "e2m1")
    return {
        "tab_words": tab_words, "tab_scales": tab_scales,
        "offs": striped(np.random.permutation(T)[:S]),
        "pos1": striped(np.random.permutation(S)[:P]),
        "w1": (0.52 * n((K, H)) / np.sqrt(K) / s).astype(np.float32),
        "expo": n((H, S)).astype(np.float32),
        "gain": (np.exp(0.3 * n(H)) * u[:, 0]).astype(np.float32),
        "w4_words": w4_words, "w4_scales": w4_scales,
        "skip": (np.exp(0.3 * n(H)) / u[:, 0]).astype(np.float32),
        "wgo": np.exp(0.3 * n((128, P))).astype(np.float32),
    }

def reference(tab_words, tab_scales, offs, pos1, w1, expo, gain, w4_words, w4_scales, skip, wgo):
    v = unpack_weight(tab_words, tab_scales, "e4m3")[:, unstriped(offs)]
    w4 = unpack_weight(w4_words, w4_scales, "e2m1")
    d = mxq(f64(w1), 0, "e4m3").T @ v
    fade = np.exp(-np.abs(d))
    h = f64(gain)[:, None] * (np.sin(d) + f64(expo) * fade)
    x = mxq(h[:, unstriped(pos1)], 0, "e4m3")
    y = np.tanh(w4.T @ x)
    out = f64(skip)[:, None] * h
    out[:, unstriped(pos1)] = np.tile(f64(wgo), (H // 128, 1)) * y
    return out

@@ -1,0 +1,253 @@
+import math
+from contextlib import ExitStack
+
+import concourse.mybir as mybir
+
+K, T, S, H, PICKS = 1536, 4096, 1024, 1024, 512
+FLOPS = 2 * K * H * S + 2 * H * H * PICKS
+
+F32 = mybir.dt.float32
+BF16 = mybir.dt.bfloat16
+I32 = mybir.dt.int32
+U32 = mybir.dt.uint32
+U16 = mybir.dt.uint16
+U8 = mybir.dt.uint8
+FP8X4 = mybir.dt.float8_e4m3fn_x4
+FP4X4 = mybir.dt.float4_e2m1fn_x4
+ALU = mybir.AluOpType
+ACT = mybir.ActivationFunctionType
+
+P = 128
+PACK = 4
+PASS = P * PACK
+BANK = 512
+K_PASSES = K // PASS
+H_PASSES = H // PASS
+TURN = 2.0 * math.pi
+
+
+def tile_list_burst_tile_merger_kernel(
+    tc, tab_words, tab_scales, offs, pos1, w1, expo, gain, w4_words, w4_scales, skip, wgo, out
+):
+    nc = tc.nc
+    expo_rows = expo.rearrange("(b p t) j -> b t p j", p=P, t=PACK)
+    out_rows = out.rearrange("(b p t) j -> b t p j", p=P, t=PACK)
+    row_tiles = [(b, t) for b in range(H_PASSES) for t in range(PACK)]
+    halves = [slice(c, c + BANK) for c in range(0, S, BANK)]
+
+    with ExitStack() as ctx:
+        keep = ctx.enter_context(tc.tile_pool(name="keep", bufs=1))
+        psum = ctx.enter_context(tc.psum_pool(name="psum", bufs=8))
+
+        tile_list = keep.tile([P, S // 16], U16, name="tile_list")
+        blur_list = keep.tile([P, PICKS // 16], U16, name="blur_list")
+
+        w4_codes = keep.tile([P, H_PASSES, H_PASSES, PACK, P, 2], U8, name="w4_codes", align_bytes=64)
+        w4_plane = keep.tile([P, H_PASSES, H_PASSES, PACK, P], U8, name="w4_plane", align_bytes=64)
+        v_codes = [keep.tile([P, S], U32, name=f"v_codes{a}", align_bytes=64) for a in range(K_PASSES)]
+        v_plane = keep.tile([P, S], U8, name="v_plane", align_bytes=64)
+        w1_raw, w1_bf16, w1_codes, w1_plane = {}, {}, {}, {}
+
+        def load_w1(a, b):
+            w1_raw[a, b] = keep.tile([P, PACK, PASS], F32, name=f"w1_raw{a}{b}")
+            rows = w1[a * PASS : (a + 1) * PASS, b * PASS : (b + 1) * PASS]
+            nc.sync.dma_start(w1_raw[a, b][:], rows.rearrange("(p j) c -> p j c", j=PACK))
+
+        def w1_views(a, b):
+            w1_bf16[a, b] = keep.tile([P, PACK * PASS], BF16, name="w1_bf16", bufs=3, align_bytes=64)
+            dst = w1_bf16[a, b][:].rearrange("p (t m j) -> p m t j", t=PACK, j=PACK)
+            src = w1_raw[a, b][:].rearrange("p j (m t) -> p m t j", t=PACK)
+            return dst, src
+
+        def quantize_w1(a, b):
+            w1_codes[a, b] = keep.tile([P, PASS], U32, name=f"w1_codes{a}{b}", align_bytes=64)
+            w1_plane[a, b] = keep.tile([P, PASS], U8, name=f"w1_plane{a}{b}", align_bytes=64)
+            nc.vector.quantize_mx(w1_codes[a, b][:].bitcast(FP8X4), w1_plane[a, b][:], w1_bf16[a, b][:])
+
+        d = {}
+
+        def first_product(a, b, t, half):
+            if a == 0:
+                d[b, t, half] = psum.tile([P, BANK], F32, name="bank")
+            rows = slice(t * P, (t + 1) * P)
+            nc.tensor.matmul_mx(
+                d[b, t, half][:],
+                lhsT=w1_codes[a, b][:, rows].bitcast(FP8X4),
+                lhsT_scale=w1_plane[a, b][:, rows],
+                rhs=v_codes[a][:, halves[half]].bitcast(FP8X4),
+                rhs_scale=v_plane[PACK * a : P, halves[half]],
+                start=(a == 0),
+                stop=(a == K_PASSES - 1),
+            )
+
+        with tc.tile_pool(name="table", bufs=1) as table:
+            tab_plane = table.tile([P, T // 4], I32, name="tab_plane")
+            w4_plane_raw = table.tile([P, H_PASSES, H], U8, name="w4_plane_raw")
+            w4_raw = table.tile([P, H_PASSES, 2 * H], U8, name="w4_raw")
+            nc.vector.memset(tab_plane[:], 0)
+            nc.gpsimd.memset(w4_plane_raw[:].bitcast(I32), 0)
+            tab = [table.tile([P, T], I32, name=f"tab{a}") for a in range(K_PASSES)]
+
+            def load_table(a):
+                nc.sync.dma_start(tab[a][:], tab_words[a].rearrange("p t i -> p (t i)").bitcast(I32))
+
+            load_table(0)
+            for q in range(4):
+                nc.sync.dma_start(
+                    tab_plane[32 * q : 32 * q + 4 * K_PASSES, :], tab_scales[:, 4 * q : 4 * q + 4, :].bitcast(I32)
+                )
+            nc.sync.dma_start(tile_list[:], offs)
+            load_w1(0, 0)
+            nc.sync.dma_start(w4_raw[:].bitcast(I32), w4_words.rearrange("a p c -> p a c").bitcast(I32))
+            load_table(1)
+            for q in range(4):
+                nc.sync.dma_start(
+                    w4_plane_raw[32 * q : 32 * q + 4].bitcast(I32),
+                    w4_scales[:, 4 * q : 4 * q + 4, :].rearrange("a r n -> r a n").bitcast(I32),
+                )
+            load_w1(1, 0)
+            load_w1(2, 0)
+            load_table(2)
+            for a in range(K_PASSES):
+                load_w1(a, 1)
+
+            nc.vector.tensor_copy(
+                w4_codes[:].rearrange("p a b t m e -> p (a b) t m e"),
+                w4_raw[:].rearrange("p a (b m t e) -> p (a b) t m e", b=H_PASSES, t=PACK, e=2),
+            )
+            nc.vector.tensor_copy(
+                w4_plane[:].rearrange("p a b t m -> p (a b) t m"),
+                w4_plane_raw[:].rearrange("p a (b m t) -> p (a b) t m", b=H_PASSES, t=PACK),
+            )
+            nc.vector.tensor_copy(v_plane[:], tab_plane[:].bitcast(U8).indirect(tile_list[:]))
+            for a in range(K_PASSES):
+                dst, src = w1_views(a, 0)
+                nc.scalar.copy(dst, src)
+                quantize_w1(a, 0)
+                window = tab[a][:].bitcast(U32)
+                if a < K_PASSES - 1:
+                    nc.vector.tensor_copy(v_codes[a][:], window.indirect(tile_list[:]))
+                else:
+                    for half, cols in enumerate(halves):
+                        entries = tile_list[:, cols.start // 16 : cols.stop // 16]
+                        nc.vector.tensor_copy(v_codes[a][:, cols], window.indirect(entries))
+                for t in range(PACK):
+                    for half in range(len(halves)):
+                        first_product(a, 0, t, half)
+
+        late = ctx.enter_context(tc.tile_pool(name="late", bufs=1))
+
+        expo_sb = {}
+        for b, t in row_tiles:
+            expo_sb[b, t] = keep.tile([P, S], F32, name="expo_sb", bufs=PACK)
+            nc.sync.dma_start(expo_sb[b, t][:], expo_rows[b, t])
+            if (b, t) == (0, PACK - 1):
+                gain_sb = keep.tile([P, H_PASSES, PACK], F32, name="gain_sb")
+                skip_sb = keep.tile([P, H_PASSES, PACK], F32, name="skip_sb")
+                nc.sync.dma_start(blur_list[:], pos1)
+                nc.sync.dma_start(gain_sb[:], gain.rearrange("(b p t) -> p b t", p=P, t=PACK))
+                nc.sync.dma_start(skip_sb[:], skip.rearrange("(b p t) -> p b t", p=P, t=PACK))
+                wgo_sb = late.tile([P, PACK, PICKS], F32, name="wgo_sb")
+                for q in range(4):
+                    nc.sync.dma_start(wgo_sb[32 * q : 32 * q + 32], wgo.rearrange("(p t) m -> p t m", t=PACK))
+
+        fade, wave = {}, {}
+
+        def read_banks(b, t):
+            pool = keep if b == 0 else late
+            fade[b, t] = pool.tile([P, S], F32, name=f"fade{b}{t}")
+            wave[b, t] = keep.tile([P, S], F32, name="wave", bufs=len(row_tiles))
+            turns = []
+            for half in range(len(halves)):
+                whole = keep.tile([P, BANK], I32, name="whole", bufs=3)
+                nc.vector.tensor_scalar(whole[:], d[b, t, half][:], 1.0 / TURN, 1.0, ALU.mult, ALU.add)
+                turns.append(whole)
+            for half, cols in enumerate(halves):
+                nc.vector.scalar_tensor_tensor(
+                    wave[b, t][:, cols], d[b, t, half][:], 1.0 / TURN, turns[half][:], ALU.mult, ALU.subtract
+                )
+            for half, cols in enumerate(halves):
+                nc.scalar.activation(fade[b, t][:, cols], d[b, t, half][:], ACT.Abs)
+            nc.scalar.activation(fade[b, t][:], fade[b, t][:], ACT.Exp, scale=-1.0)
+
+        for t in range(PACK):
+            read_banks(0, t)
+        for a in range(K_PASSES):
+            dst, src = w1_views(a, 1)
+            nc.gpsimd.tensor_scalar(dst, src, 1.0, 0.0, ALU.mult, ALU.add)
+        for a in range(K_PASSES):
+            quantize_w1(a, 1)
+        for t in range(PACK):
+            for half in range(len(halves)):
+                for a in range(K_PASSES):
+                    first_product(a, 1, t, half)
+
+        offset, tone = {}, {}
+        offset[0, 0] = w1_bf16[K_PASSES - 1, 1][:].bitcast(F32)
+        tone[0, 0] = fade[0, PACK - 1]
+        for t in range(1, PACK):
+            offset[0, t] = fade[0, t - 1][:]
+            tone[0, t] = fade[0, t - 1]
+        for t in range(PACK):
+            nc.gpsimd.tensor_tensor(offset[0, t], fade[0, t][:], expo_sb[0, t][:], ALU.mult)
+
+        for t in range(PACK):
+            read_banks(1, t)
+        for t in range(PACK):
+            offset[1, t] = fade[1, t][:]
+            tone[1, t] = fade[1, t]
+            nc.vector.scalar_tensor_tensor(
+                offset[1, t], fade[1, t][:], gain_sb[:, 1, t : t + 1], expo_sb[1, t][:], ALU.mult, ALU.mult
+            )
+        for b, t in row_tiles:
+            nc.scalar.activation(wave[b, t][:], wave[b, t][:], ACT.Sin, scale=TURN, bias=TURN)
+
+        skip_gain = keep.tile([P, PACK], F32, name="skip_gain")
+        nc.vector.tensor_tensor(skip_gain[:], skip_sb[:, 0, :], gain_sb[:, 0, :], ALU.mult)
+
+        x_codes, x_plane, page = {}, {}, {}
+        for b in range(H_PASSES):
+            picked = late.tile([P, PACK, PICKS], F32, name=f"picked{b}")
+            for t in range(PACK):
+                if b == 0:
+                    nc.vector.tensor_tensor(tone[b, t][:], wave[b, t][:], offset[b, t], ALU.add)
+                else:
+                    nc.vector.scalar_tensor_tensor(
+                        tone[b, t][:], wave[b, t][:], gain_sb[:, b, t : t + 1], offset[b, t], ALU.mult, ALU.add
+                    )
+                nc.vector.tensor_copy(picked[:, t, :], tone[b, t][:].indirect(blur_list[:]))
+            x_bf16 = late.tile([P, PICKS, PACK], BF16, name=f"x_bf16{b}", align_bytes=64)
+            if b == 0:
+                rounded = late.tile([P, PACK, PICKS], BF16, name="rounded")
+                for t in range(PACK):
+                    nc.scalar.activation(rounded[:, t, :], picked[:, t, :], ACT.Copy, scale=gain_sb[:, b, t : t + 1])
+                nc.scalar.copy(x_bf16[:], rounded[:].rearrange("p t m -> p m t"))
+            else:
+                nc.vector.tensor_copy(x_bf16[:], picked[:].rearrange("p t m -> p m t"))
+            x_codes[b] = late.tile([P, PICKS], U32, name=f"x_codes{b}", align_bytes=64)
+            x_plane[b] = late.tile([P, PICKS], U8, name=f"x_plane{b}", align_bytes=64)
+            nc.vector.quantize_mx(x_codes[b][:].bitcast(FP8X4), x_plane[b][:], x_bf16[:].rearrange("p m t -> p (m t)"))
+            for t in range(PACK):
+                page[b, t] = keep.tile([P, S], F32, name="wave", bufs=len(row_tiles))
+                factor = skip_gain[:, t : t + 1] if b == 0 else skip_sb[:, b, t : t + 1]
+                nc.scalar.activation(page[b, t][:], tone[b, t][:], ACT.Copy, scale=factor)
+
+        y = {}
+        for a in range(H_PASSES):
+            for b, t in row_tiles:
+                if a == 0:
+                    y[b, t] = psum.tile([P, PICKS], F32, name="bank")
+                nc.tensor.matmul_mx(
+                    y[b, t][:],
+                    lhsT=w4_codes[:, a, b, t].rearrange("p m e -> p (m e)").bitcast(FP4X4),
+                    lhsT_scale=w4_plane[:, a, b, t, :],
+                    rhs=x_codes[a][:].bitcast(FP8X4),
+                    rhs_scale=x_plane[a][:],
+                    start=(a == 0),
+                    stop=(a == H_PASSES - 1),
+                )
+        for b, t in row_tiles:
+            mapped = late.tile([P, PICKS], F32, name="mapped", bufs=2)
+            nc.scalar.activation(mapped[:], y[b, t][:], ACT.Tanh)
+            nc.vector.tensor_tensor(page[b, t][:].indirect(blur_list[:]), mapped[:], wgo_sb[:, t, :], ALU.mult)
+            nc.sync.dma_start(out_rows[b, t], page[b, t][:])

@@ -99,14 +99,14 @@ def tile_list_burst_tile_merger_kernel(
             nc.sync.dma_start(tile_list[:], offs)
             load_w1(0, 0)
             nc.sync.dma_start(w4_raw[:].bitcast(I32), w4_words.rearrange("a p c -> p a c").bitcast(I32))
-            load_table(1)
+            load_w1(1, 0)
             for q in range(4):
                 nc.sync.dma_start(
                     w4_plane_raw[32 * q : 32 * q + 4].bitcast(I32),
                     w4_scales[:, 4 * q : 4 * q + 4, :].rearrange("a r n -> r a n").bitcast(I32),
                 )
-            load_w1(1, 0)
             load_w1(2, 0)
+            load_table(1)
             load_table(2)
             for a in range(K_PASSES):
                 load_w1(a, 1)
@@ -153,30 +153,45 @@ def tile_list_burst_tile_merger_kernel(
 
         fade, wave = {}, {}
 
-        def read_banks(b, t):
-            pool = keep if b == 0 else late
-            fade[b, t] = pool.tile([P, S], F32, name=f"fade{b}{t}")
-            wave[b, t] = keep.tile([P, S], F32, name="wave", bufs=len(row_tiles))
-            turns = []
+        turns = {}
+
+        def count_turns(b, t):
             for half in range(len(halves)):
-                whole = keep.tile([P, BANK], I32, name="whole", bufs=3)
-                nc.vector.tensor_scalar(whole[:], d[b, t, half][:], 1.0 / TURN, 1.0, ALU.mult, ALU.add)
-                turns.append(whole)
+                turns[b, t, half] = keep.tile([P, BANK], I32, name="turns", bufs=3)
+                nc.vector.tensor_scalar(turns[b, t, half][:], d[b, t, half][:], 1.0 / TURN, None, ALU.mult)
+
+        def reduce_range(b, t):
+            wave[b, t] = keep.tile([P, S], F32, name="wave", bufs=len(row_tiles))
             for half, cols in enumerate(halves):
                 nc.vector.scalar_tensor_tensor(
-                    wave[b, t][:, cols], d[b, t, half][:], 1.0 / TURN, turns[half][:], ALU.mult, ALU.subtract
+                    wave[b, t][:, cols], d[b, t, half][:], 1.0 / TURN, turns[b, t, half][:], ALU.mult, ALU.subtract
                 )
+
+        def magnitude(b, t):
+            pool = keep if b == 0 else late
+            fade[b, t] = pool.tile([P, S], F32, name=f"fade{b}{t}")
             for half, cols in enumerate(halves):
                 nc.scalar.activation(fade[b, t][:, cols], d[b, t, half][:], ACT.Abs)
+
+        def decay(b, t):
             nc.scalar.activation(fade[b, t][:], fade[b, t][:], ACT.Exp, scale=-1.0)
 
         for t in range(PACK):
-            read_banks(0, t)
+            magnitude(0, t)
         for a in range(K_PASSES):
             dst, src = w1_views(a, 1)
-            nc.gpsimd.tensor_scalar(dst, src, 1.0, 0.0, ALU.mult, ALU.add)
-        for a in range(K_PASSES):
-            quantize_w1(a, 1)
+            if a < K_PASSES - 1:
+                nc.gpsimd.tensor_scalar(dst, src, 1.0, 0.0, ALU.mult, ALU.add)
+            else:
+                nc.scalar.copy(dst, src)
+        for t in range(PACK):
+            decay(0, t)
+        for t in range(PACK):
+            count_turns(0, t)
+            if t == PACK - 1:
+                for a in range(K_PASSES):
+                    quantize_w1(a, 1)
+            reduce_range(0, t)
         for t in range(PACK):
             for half in range(len(halves)):
                 for a in range(K_PASSES):
@@ -192,7 +207,10 @@ def tile_list_burst_tile_merger_kernel(
             nc.gpsimd.tensor_tensor(offset[0, t], fade[0, t][:], expo_sb[0, t][:], ALU.mult)
 
         for t in range(PACK):
-            read_banks(1, t)
+            count_turns(1, t)
+            reduce_range(1, t)
+            magnitude(1, t)
+            decay(1, t)
         for t in range(PACK):
             offset[1, t] = fade[1, t][:]
             tone[1, t] = fade[1, t]
@@ -200,54 +218,66 @@ def tile_list_burst_tile_merger_kernel(
                 offset[1, t], fade[1, t][:], gain_sb[:, 1, t : t + 1], expo_sb[1, t][:], ALU.mult, ALU.mult
             )
         for b, t in row_tiles:
-            nc.scalar.activation(wave[b, t][:], wave[b, t][:], ACT.Sin, scale=TURN, bias=TURN)
+            nc.scalar.activation(wave[b, t][:], wave[b, t][:], ACT.Sin, scale=TURN)
 
         skip_gain = keep.tile([P, PACK], F32, name="skip_gain")
         nc.vector.tensor_tensor(skip_gain[:], skip_sb[:, 0, :], gain_sb[:, 0, :], ALU.mult)
 
-        x_codes, x_plane, page = {}, {}, {}
-        for b in range(H_PASSES):
-            picked = late.tile([P, PACK, PICKS], F32, name=f"picked{b}")
-            for t in range(PACK):
-                if b == 0:
-                    nc.vector.tensor_tensor(tone[b, t][:], wave[b, t][:], offset[b, t], ALU.add)
-                else:
-                    nc.vector.scalar_tensor_tensor(
-                        tone[b, t][:], wave[b, t][:], gain_sb[:, b, t : t + 1], offset[b, t], ALU.mult, ALU.add
-                    )
-                nc.vector.tensor_copy(picked[:, t, :], tone[b, t][:].indirect(blur_list[:]))
-            x_bf16 = late.tile([P, PICKS, PACK], BF16, name=f"x_bf16{b}", align_bytes=64)
-            if b == 0:
-                rounded = late.tile([P, PACK, PICKS], BF16, name="rounded")
-                for t in range(PACK):
-                    nc.scalar.activation(rounded[:, t, :], picked[:, t, :], ACT.Copy, scale=gain_sb[:, b, t : t + 1])
-                nc.scalar.copy(x_bf16[:], rounded[:].rearrange("p t m -> p m t"))
-            else:
-                nc.vector.tensor_copy(x_bf16[:], picked[:].rearrange("p t m -> p m t"))
-            x_codes[b] = late.tile([P, PICKS], U32, name=f"x_codes{b}", align_bytes=64)
-            x_plane[b] = late.tile([P, PICKS], U8, name=f"x_plane{b}", align_bytes=64)
-            nc.vector.quantize_mx(x_codes[b][:].bitcast(FP8X4), x_plane[b][:], x_bf16[:].rearrange("p m t -> p (m t)"))
-            for t in range(PACK):
-                page[b, t] = keep.tile([P, S], F32, name="wave", bufs=len(row_tiles))
-                factor = skip_gain[:, t : t + 1] if b == 0 else skip_sb[:, b, t : t + 1]
-                nc.scalar.activation(page[b, t][:], tone[b, t][:], ACT.Copy, scale=factor)
+        picked = [late.tile([P, PACK, PICKS], F32, name=f"picked{b}") for b in range(H_PASSES)]
+        x_bf16 = [late.tile([P, PICKS, PACK], BF16, name=f"x_bf16{b}", align_bytes=64) for b in range(H_PASSES)]
+        x_codes = [late.tile([P, PICKS], U32, name=f"x_codes{b}", align_bytes=64) for b in range(H_PASSES)]
+        x_plane = [late.tile([P, PICKS], U8, name=f"x_plane{b}", align_bytes=64) for b in range(H_PASSES)]
+        pick_halves = [slice(0, PICKS // 2), slice(PICKS // 2, PICKS)]
 
-        y = {}
-        for a in range(H_PASSES):
-            for b, t in row_tiles:
-                if a == 0:
-                    y[b, t] = psum.tile([P, PICKS], F32, name="bank")
-                nc.tensor.matmul_mx(
-                    y[b, t][:],
-                    lhsT=w4_codes[:, a, b, t].rearrange("p m e -> p (m e)").bitcast(FP4X4),
-                    lhsT_scale=w4_plane[:, a, b, t, :],
-                    rhs=x_codes[a][:].bitcast(FP8X4),
-                    rhs_scale=x_plane[a][:],
-                    start=(a == 0),
-                    stop=(a == H_PASSES - 1),
+        def add_terms(b, t):
+            if b == 0:
+                nc.vector.tensor_tensor(tone[b, t][:], wave[b, t][:], offset[b, t], ALU.add)
+            else:
+                nc.vector.scalar_tensor_tensor(
+                    tone[b, t][:], wave[b, t][:], gain_sb[:, b, t : t + 1], offset[b, t], ALU.mult, ALU.add
                 )
-        for b, t in row_tiles:
-            mapped = late.tile([P, PICKS], F32, name="mapped", bufs=2)
-            nc.scalar.activation(mapped[:], y[b, t][:], ACT.Tanh)
-            nc.vector.tensor_tensor(page[b, t][:].indirect(blur_list[:]), mapped[:], wgo_sb[:, t, :], ALU.mult)
-            nc.sync.dma_start(out_rows[b, t], page[b, t][:])
+
+        def quantize_x(b, cols):
+            nc.vector.quantize_mx(
+                x_codes[b][:, cols].bitcast(FP8X4),
+                x_plane[b][:, cols],
+                x_bf16[b][:, cols, :].rearrange("p m t -> p (m t)"),
+            )
+
+        add_terms(*row_tiles[0])
+        for i, (b, t) in enumerate(row_tiles):
+            if i + 1 < len(row_tiles):
+                add_terms(*row_tiles[i + 1])
+            nc.vector.tensor_copy(picked[b][:, t, :], tone[b, t][:].indirect(blur_list[:]))
+            if (b, t) == (0, PACK - 1):
+                rounded = late.tile([P, PACK, PICKS], BF16, name="rounded")
+                for u in range(PACK):
+                    nc.scalar.activation(rounded[:, u, :], picked[0][:, u, :], ACT.Copy, scale=gain_sb[:, 0, u : u + 1])
+                nc.scalar.copy(x_bf16[0][:], rounded[:].rearrange("p t m -> p m t"))
+                quantize_x(0, slice(0, PICKS))
+        for cols in pick_halves:
+            nc.vector.tensor_copy(x_bf16[1][:, cols, :], picked[1][:, :, cols].rearrange("p t m -> p m t"))
+            quantize_x(1, cols)
+
+        for i, (b, t) in enumerate(row_tiles):
+            page = keep.tile([P, S], F32, name="wave", bufs=len(row_tiles))
+            factor = skip_gain[:, t : t + 1] if b == 0 else skip_sb[:, b, t : t + 1]
+            nc.scalar.activation(page[:], tone[b, t][:], ACT.Copy, scale=factor)
+            for cols in pick_halves if i == 0 else [slice(0, PICKS)]:
+                width = cols.stop - cols.start
+                y = psum.tile([P, BANK], F32, name="bank")
+                for a in range(H_PASSES):
+                    nc.tensor.matmul_mx(
+                        y[:, :width],
+                        lhsT=w4_codes[:, a, b, t].rearrange("p m e -> p (m e)").bitcast(FP4X4),
+                        lhsT_scale=w4_plane[:, a, b, t, :],
+                        rhs=x_codes[a][:, cols].bitcast(FP8X4),
+                        rhs_scale=x_plane[a][:, cols],
+                        start=(a == 0),
+                        stop=(a == H_PASSES - 1),
+                    )
+                mapped = late.tile([P, PICKS], F32, name="mapped", bufs=2)
+                nc.scalar.activation(mapped[:, :width], y[:, :width], ACT.Tanh)
+                entries = blur_list[:, cols.start // 16 : cols.stop // 16]
+                nc.vector.tensor_tensor(page[:].indirect(entries), mapped[:, :width], wgo_sb[:, t, cols], ALU.mult)
+            nc.sync.dma_start(out_rows[b, t], page[:])

@@ -111,14 +111,6 @@ def tile_list_burst_tile_merger_kernel(
             for a in range(K_PASSES):
                 load_w1(a, 1)
 
-            nc.vector.tensor_copy(
-                w4_codes[:].rearrange("p a b t m e -> p (a b) t m e"),
-                w4_raw[:].rearrange("p a (b m t e) -> p (a b) t m e", b=H_PASSES, t=PACK, e=2),
-            )
-            nc.vector.tensor_copy(
-                w4_plane[:].rearrange("p a b t m -> p (a b) t m"),
-                w4_plane_raw[:].rearrange("p a (b m t) -> p (a b) t m", b=H_PASSES, t=PACK),
-            )
             nc.vector.tensor_copy(v_plane[:], tab_plane[:].bitcast(U8).indirect(tile_list[:]))
             for a in range(K_PASSES):
                 dst, src = w1_views(a, 0)
@@ -134,6 +126,15 @@ def tile_list_burst_tile_merger_kernel(
                 for t in range(PACK):
                     for half in range(len(halves)):
                         first_product(a, 0, t, half)
+                if a == 0:
+                    nc.vector.tensor_copy(
+                        w4_codes[:].rearrange("p a b t m e -> p (a b) t m e"),
+                        w4_raw[:].rearrange("p a (b m t e) -> p (a b) t m e", b=H_PASSES, t=PACK, e=2),
+                    )
+                    nc.vector.tensor_copy(
+                        w4_plane[:].rearrange("p a b t m -> p (a b) t m"),
+                        w4_plane_raw[:].rearrange("p a (b m t) -> p (a b) t m", b=H_PASSES, t=PACK),
+                    )
 
         late = ctx.enter_context(tc.tile_pool(name="late", bufs=1))
 
@@ -183,14 +184,17 @@ def tile_list_burst_tile_merger_kernel(
             if a < K_PASSES - 1:
                 nc.gpsimd.tensor_scalar(dst, src, 1.0, 0.0, ALU.mult, ALU.add)
             else:
-                nc.scalar.copy(dst, src)
+                nc.gpsimd.tensor_scalar(dst[:, : P // 2], src[:, : P // 2], 1.0, 0.0, ALU.mult, ALU.add)
+                nc.scalar.copy(dst[:, P // 2 :], src[:, P // 2 :])
         for t in range(PACK):
             decay(0, t)
         for t in range(PACK):
+            if t == PACK - 1:
+                for a in range(K_PASSES - 1):
+                    quantize_w1(a, 1)
             count_turns(0, t)
             if t == PACK - 1:
-                for a in range(K_PASSES):
-                    quantize_w1(a, 1)
+                quantize_w1(K_PASSES - 1, 1)
             reduce_range(0, t)
         for t in range(PACK):
             for half in range(len(halves)):

@@ -21,9 +21,15 @@ P = 128
 PACK = 4
 PASS = P * PACK
 BANK = 512
+BANKS = 8
+QUADS = 4
+QUAD = P // QUADS
+QUAD_BLOCKS = 4
+LIST_ROWS = 16
 K_PASSES = K // PASS
 H_PASSES = H // PASS
 TURN = 2.0 * math.pi
+EXPO_BUFS = 6
 
 
 def tile_list_burst_tile_merger_kernel(
@@ -37,10 +43,10 @@ def tile_list_burst_tile_merger_kernel(
 
     with ExitStack() as ctx:
         keep = ctx.enter_context(tc.tile_pool(name="keep", bufs=1))
-        psum = ctx.enter_context(tc.psum_pool(name="psum", bufs=8))
+        psum = ctx.enter_context(tc.psum_pool(name="psum", bufs=BANKS))
 
-        tile_list = keep.tile([P, S // 16], U16, name="tile_list")
-        blur_list = keep.tile([P, PICKS // 16], U16, name="blur_list")
+        tile_list = keep.tile([P, S // LIST_ROWS], U16, name="tile_list")
+        blur_list = keep.tile([P, PICKS // LIST_ROWS], U16, name="blur_list")
 
         w4_codes = keep.tile([P, H_PASSES, H_PASSES, PACK, P, 2], U8, name="w4_codes", align_bytes=64)
         w4_plane = keep.tile([P, H_PASSES, H_PASSES, PACK, P], U8, name="w4_plane", align_bytes=64)
@@ -54,7 +60,7 @@ def tile_list_burst_tile_merger_kernel(
             nc.sync.dma_start(w1_raw[a, b][:], rows.rearrange("(p j) c -> p j c", j=PACK))
 
         def w1_views(a, b):
-            w1_bf16[a, b] = keep.tile([P, PACK * PASS], BF16, name="w1_bf16", bufs=3, align_bytes=64)
+            w1_bf16[a, b] = keep.tile([P, PACK * PASS], BF16, name="w1_bf16", bufs=K_PASSES, align_bytes=64)
             dst = w1_bf16[a, b][:].rearrange("p (t m j) -> p m t j", t=PACK, j=PACK)
             src = w1_raw[a, b][:].rearrange("p j (m t) -> p m t j", t=PACK)
             return dst, src
@@ -75,7 +81,7 @@ def tile_list_burst_tile_merger_kernel(
                 lhsT=w1_codes[a, b][:, rows].bitcast(FP8X4),
                 lhsT_scale=w1_plane[a, b][:, rows],
                 rhs=v_codes[a][:, halves[half]].bitcast(FP8X4),
-                rhs_scale=v_plane[PACK * a : P, halves[half]],
+                rhs_scale=v_plane[QUAD_BLOCKS * a : P, halves[half]],
                 start=(a == 0),
                 stop=(a == K_PASSES - 1),
             )
@@ -92,18 +98,19 @@ def tile_list_burst_tile_merger_kernel(
                 nc.sync.dma_start(tab[a][:], tab_words[a].rearrange("p t i -> p (t i)").bitcast(I32))
 
             load_table(0)
-            for q in range(4):
+            for q in range(QUADS):
                 nc.sync.dma_start(
-                    tab_plane[32 * q : 32 * q + 4 * K_PASSES, :], tab_scales[:, 4 * q : 4 * q + 4, :].bitcast(I32)
+                    tab_plane[QUAD * q : QUAD * q + QUAD_BLOCKS * K_PASSES, :],
+                    tab_scales[:, QUAD_BLOCKS * q : QUAD_BLOCKS * (q + 1), :].bitcast(I32),
                 )
             nc.sync.dma_start(tile_list[:], offs)
             load_w1(0, 0)
             nc.sync.dma_start(w4_raw[:].bitcast(I32), w4_words.rearrange("a p c -> p a c").bitcast(I32))
             load_w1(1, 0)
-            for q in range(4):
+            for q in range(QUADS):
                 nc.sync.dma_start(
-                    w4_plane_raw[32 * q : 32 * q + 4].bitcast(I32),
-                    w4_scales[:, 4 * q : 4 * q + 4, :].rearrange("a r n -> r a n").bitcast(I32),
+                    w4_plane_raw[QUAD * q : QUAD * q + QUAD_BLOCKS].bitcast(I32),
+                    w4_scales[:, QUAD_BLOCKS * q : QUAD_BLOCKS * (q + 1), :].rearrange("a r n -> r a n").bitcast(I32),
                 )
             load_w1(2, 0)
             load_table(1)
@@ -120,8 +127,8 @@ def tile_list_burst_tile_merger_kernel(
                 if a < K_PASSES - 1:
                     nc.vector.tensor_copy(v_codes[a][:], window.indirect(tile_list[:]))
                 else:
-                    for half, cols in enumerate(halves):
-                        entries = tile_list[:, cols.start // 16 : cols.stop // 16]
+                    for cols in halves:
+                        entries = tile_list[:, cols.start // LIST_ROWS : cols.stop // LIST_ROWS]
                         nc.vector.tensor_copy(v_codes[a][:, cols], window.indirect(entries))
                 for t in range(PACK):
                     for half in range(len(halves)):
@@ -140,7 +147,7 @@ def tile_list_burst_tile_merger_kernel(
 
         expo_sb = {}
         for b, t in row_tiles:
-            expo_sb[b, t] = keep.tile([P, S], F32, name="expo_sb", bufs=PACK)
+            expo_sb[b, t] = keep.tile([P, S], F32, name="expo_sb", bufs=EXPO_BUFS)
             nc.sync.dma_start(expo_sb[b, t][:], expo_rows[b, t])
             if (b, t) == (0, PACK - 1):
                 gain_sb = keep.tile([P, H_PASSES, PACK], F32, name="gain_sb")
@@ -149,12 +156,10 @@ def tile_list_burst_tile_merger_kernel(
                 nc.sync.dma_start(gain_sb[:], gain.rearrange("(b p t) -> p b t", p=P, t=PACK))
                 nc.sync.dma_start(skip_sb[:], skip.rearrange("(b p t) -> p b t", p=P, t=PACK))
                 wgo_sb = late.tile([P, PACK, PICKS], F32, name="wgo_sb")
-                for q in range(4):
-                    nc.sync.dma_start(wgo_sb[32 * q : 32 * q + 32], wgo.rearrange("(p t) m -> p t m", t=PACK))
+                for q in range(QUADS):
+                    nc.sync.dma_start(wgo_sb[QUAD * q : QUAD * (q + 1)], wgo.rearrange("(p t) m -> p t m", t=PACK))
 
-        fade, wave = {}, {}
-
-        turns = {}
+        fade, wave, turns = {}, {}, {}
 
         def count_turns(b, t):
             for half in range(len(halves)):
@@ -282,6 +287,6 @@ def tile_list_burst_tile_merger_kernel(
                     )
                 mapped = late.tile([P, PICKS], F32, name="mapped", bufs=2)
                 nc.scalar.activation(mapped[:, :width], y[:, :width], ACT.Tanh)
-                entries = blur_list[:, cols.start // 16 : cols.stop // 16]
+                entries = blur_list[:, cols.start // LIST_ROWS : cols.stop // LIST_ROWS]
                 nc.vector.tensor_tensor(page[:].indirect(entries), mapped[:, :width], wgo_sb[:, t, cols], ALU.mult)
             nc.sync.dma_start(out_rows[b, t], page[:])

import math
from contextlib import ExitStack

import concourse.mybir as mybir

K, T, S, H, PICKS = 1536, 4096, 1024, 1024, 512
FLOPS = 2 * K * H * S + 2 * H * H * PICKS

F32 = mybir.dt.float32
BF16 = mybir.dt.bfloat16
I32 = mybir.dt.int32
U32 = mybir.dt.uint32
U16 = mybir.dt.uint16
U8 = mybir.dt.uint8
FP8X4 = mybir.dt.float8_e4m3fn_x4
FP4X4 = mybir.dt.float4_e2m1fn_x4
ALU = mybir.AluOpType
ACT = mybir.ActivationFunctionType

P = 128
PACK = 4
PASS = P * PACK
BANK = 512
BANKS = 8
QUADS = 4
QUAD = P // QUADS
QUAD_BLOCKS = 4
LIST_ROWS = 16
K_PASSES = K // PASS
H_PASSES = H // PASS
TURN = 2.0 * math.pi
EXPO_BUFS = 6


def tile_list_burst_tile_merger_kernel(
    tc, tab_words, tab_scales, offs, pos1, w1, expo, gain, w4_words, w4_scales, skip, wgo, out
):
    nc = tc.nc
    expo_rows = expo.rearrange("(b p t) j -> b t p j", p=P, t=PACK)
    out_rows = out.rearrange("(b p t) j -> b t p j", p=P, t=PACK)
    row_tiles = [(b, t) for b in range(H_PASSES) for t in range(PACK)]
    halves = [slice(c, c + BANK) for c in range(0, S, BANK)]

    with ExitStack() as ctx:
        keep = ctx.enter_context(tc.tile_pool(name="keep", bufs=1))
        psum = ctx.enter_context(tc.psum_pool(name="psum", bufs=BANKS))

        tile_list = keep.tile([P, S // LIST_ROWS], U16, name="tile_list")
        blur_list = keep.tile([P, PICKS // LIST_ROWS], U16, name="blur_list")

        w4_codes = keep.tile([P, H_PASSES, H_PASSES, PACK, P, 2], U8, name="w4_codes", align_bytes=64)
        w4_plane = keep.tile([P, H_PASSES, H_PASSES, PACK, P], U8, name="w4_plane", align_bytes=64)
        v_codes = [keep.tile([P, S], U32, name=f"v_codes{a}", align_bytes=64) for a in range(K_PASSES)]
        v_plane = keep.tile([P, S], U8, name="v_plane", align_bytes=64)
        w1_raw, w1_bf16, w1_codes, w1_plane = {}, {}, {}, {}

        def load_w1(a, b):
            w1_raw[a, b] = keep.tile([P, PACK, PASS], F32, name=f"w1_raw{a}{b}")
            rows = w1[a * PASS : (a + 1) * PASS, b * PASS : (b + 1) * PASS]
            nc.sync.dma_start(w1_raw[a, b][:], rows.rearrange("(p j) c -> p j c", j=PACK))

        def w1_views(a, b):
            w1_bf16[a, b] = keep.tile([P, PACK * PASS], BF16, name="w1_bf16", bufs=K_PASSES, align_bytes=64)
            dst = w1_bf16[a, b][:].rearrange("p (t m j) -> p m t j", t=PACK, j=PACK)
            src = w1_raw[a, b][:].rearrange("p j (m t) -> p m t j", t=PACK)
            return dst, src

        def quantize_w1(a, b):
            w1_codes[a, b] = keep.tile([P, PASS], U32, name=f"w1_codes{a}{b}", align_bytes=64)
            w1_plane[a, b] = keep.tile([P, PASS], U8, name=f"w1_plane{a}{b}", align_bytes=64)
            nc.vector.quantize_mx(w1_codes[a, b][:].bitcast(FP8X4), w1_plane[a, b][:], w1_bf16[a, b][:])

        d = {}

        def first_product(a, b, t, half):
            if a == 0:
                d[b, t, half] = psum.tile([P, BANK], F32, name="bank")
            rows = slice(t * P, (t + 1) * P)
            nc.tensor.matmul_mx(
                d[b, t, half][:],
                lhsT=w1_codes[a, b][:, rows].bitcast(FP8X4),
                lhsT_scale=w1_plane[a, b][:, rows],
                rhs=v_codes[a][:, halves[half]].bitcast(FP8X4),
                rhs_scale=v_plane[QUAD_BLOCKS * a : P, halves[half]],
                start=(a == 0),
                stop=(a == K_PASSES - 1),
            )

        with tc.tile_pool(name="table", bufs=1) as table:
            tab_plane = table.tile([P, T // 4], I32, name="tab_plane")
            w4_plane_raw = table.tile([P, H_PASSES, H], U8, name="w4_plane_raw")
            w4_raw = table.tile([P, H_PASSES, 2 * H], U8, name="w4_raw")
            nc.vector.memset(tab_plane[:], 0)
            nc.gpsimd.memset(w4_plane_raw[:].bitcast(I32), 0)
            tab = [table.tile([P, T], I32, name=f"tab{a}") for a in range(K_PASSES)]

            def load_table(a):
                nc.sync.dma_start(tab[a][:], tab_words[a].rearrange("p t i -> p (t i)").bitcast(I32))

            load_table(0)
            for q in range(QUADS):
                nc.sync.dma_start(
                    tab_plane[QUAD * q : QUAD * q + QUAD_BLOCKS * K_PASSES, :],
                    tab_scales[:, QUAD_BLOCKS * q : QUAD_BLOCKS * (q + 1), :].bitcast(I32),
                )
            nc.sync.dma_start(tile_list[:], offs)
            load_w1(0, 0)
            nc.sync.dma_start(w4_raw[:].bitcast(I32), w4_words.rearrange("a p c -> p a c").bitcast(I32))
            load_w1(1, 0)
            for q in range(QUADS):
                nc.sync.dma_start(
                    w4_plane_raw[QUAD * q : QUAD * q + QUAD_BLOCKS].bitcast(I32),
                    w4_scales[:, QUAD_BLOCKS * q : QUAD_BLOCKS * (q + 1), :].rearrange("a r n -> r a n").bitcast(I32),
                )
            load_w1(2, 0)
            load_table(1)
            load_table(2)
            for a in range(K_PASSES):
                load_w1(a, 1)

            nc.vector.tensor_copy(v_plane[:], tab_plane[:].bitcast(U8).indirect(tile_list[:]))
            for a in range(K_PASSES):
                dst, src = w1_views(a, 0)
                nc.scalar.copy(dst, src)
                quantize_w1(a, 0)
                window = tab[a][:].bitcast(U32)
                if a < K_PASSES - 1:
                    nc.vector.tensor_copy(v_codes[a][:], window.indirect(tile_list[:]))
                else:
                    for cols in halves:
                        entries = tile_list[:, cols.start // LIST_ROWS : cols.stop // LIST_ROWS]
                        nc.vector.tensor_copy(v_codes[a][:, cols], window.indirect(entries))
                for t in range(PACK):
                    for half in range(len(halves)):
                        first_product(a, 0, t, half)
                if a == 0:
                    nc.vector.tensor_copy(
                        w4_codes[:].rearrange("p a b t m e -> p (a b) t m e"),
                        w4_raw[:].rearrange("p a (b m t e) -> p (a b) t m e", b=H_PASSES, t=PACK, e=2),
                    )
                    nc.vector.tensor_copy(
                        w4_plane[:].rearrange("p a b t m -> p (a b) t m"),
                        w4_plane_raw[:].rearrange("p a (b m t) -> p (a b) t m", b=H_PASSES, t=PACK),
                    )

        late = ctx.enter_context(tc.tile_pool(name="late", bufs=1))

        expo_sb = {}
        for b, t in row_tiles:
            expo_sb[b, t] = keep.tile([P, S], F32, name="expo_sb", bufs=EXPO_BUFS)
            nc.sync.dma_start(expo_sb[b, t][:], expo_rows[b, t])
            if (b, t) == (0, PACK - 1):
                gain_sb = keep.tile([P, H_PASSES, PACK], F32, name="gain_sb")
                skip_sb = keep.tile([P, H_PASSES, PACK], F32, name="skip_sb")
                nc.sync.dma_start(blur_list[:], pos1)
                nc.sync.dma_start(gain_sb[:], gain.rearrange("(b p t) -> p b t", p=P, t=PACK))
                nc.sync.dma_start(skip_sb[:], skip.rearrange("(b p t) -> p b t", p=P, t=PACK))
                wgo_sb = late.tile([P, PACK, PICKS], F32, name="wgo_sb")
                for q in range(QUADS):
                    nc.sync.dma_start(wgo_sb[QUAD * q : QUAD * (q + 1)], wgo.rearrange("(p t) m -> p t m", t=PACK))

        fade, wave, turns = {}, {}, {}

        def count_turns(b, t):
            for half in range(len(halves)):
                turns[b, t, half] = keep.tile([P, BANK], I32, name="turns", bufs=3)
                nc.vector.tensor_scalar(turns[b, t, half][:], d[b, t, half][:], 1.0 / TURN, None, ALU.mult)

        def reduce_range(b, t):
            wave[b, t] = keep.tile([P, S], F32, name="wave", bufs=len(row_tiles))
            for half, cols in enumerate(halves):
                nc.vector.scalar_tensor_tensor(
                    wave[b, t][:, cols], d[b, t, half][:], 1.0 / TURN, turns[b, t, half][:], ALU.mult, ALU.subtract
                )

        def magnitude(b, t):
            pool = keep if b == 0 else late
            fade[b, t] = pool.tile([P, S], F32, name=f"fade{b}{t}")
            for half, cols in enumerate(halves):
                nc.scalar.activation(fade[b, t][:, cols], d[b, t, half][:], ACT.Abs)

        def decay(b, t):
            nc.scalar.activation(fade[b, t][:], fade[b, t][:], ACT.Exp, scale=-1.0)

        for t in range(PACK):
            magnitude(0, t)
        for a in range(K_PASSES):
            dst, src = w1_views(a, 1)
            if a < K_PASSES - 1:
                nc.gpsimd.tensor_scalar(dst, src, 1.0, 0.0, ALU.mult, ALU.add)
            else:
                nc.gpsimd.tensor_scalar(dst[:, : P // 2], src[:, : P // 2], 1.0, 0.0, ALU.mult, ALU.add)
                nc.scalar.copy(dst[:, P // 2 :], src[:, P // 2 :])
        for t in range(PACK):
            decay(0, t)
        for t in range(PACK):
            if t == PACK - 1:
                for a in range(K_PASSES - 1):
                    quantize_w1(a, 1)
            count_turns(0, t)
            if t == PACK - 1:
                quantize_w1(K_PASSES - 1, 1)
            reduce_range(0, t)
        for t in range(PACK):
            for half in range(len(halves)):
                for a in range(K_PASSES):
                    first_product(a, 1, t, half)

        offset, tone = {}, {}
        offset[0, 0] = w1_bf16[K_PASSES - 1, 1][:].bitcast(F32)
        tone[0, 0] = fade[0, PACK - 1]
        for t in range(1, PACK):
            offset[0, t] = fade[0, t - 1][:]
            tone[0, t] = fade[0, t - 1]
        for t in range(PACK):
            nc.gpsimd.tensor_tensor(offset[0, t], fade[0, t][:], expo_sb[0, t][:], ALU.mult)

        for t in range(PACK):
            count_turns(1, t)
            reduce_range(1, t)
            magnitude(1, t)
            decay(1, t)
        for t in range(PACK):
            offset[1, t] = fade[1, t][:]
            tone[1, t] = fade[1, t]
            nc.vector.scalar_tensor_tensor(
                offset[1, t], fade[1, t][:], gain_sb[:, 1, t : t + 1], expo_sb[1, t][:], ALU.mult, ALU.mult
            )
        for b, t in row_tiles:
            nc.scalar.activation(wave[b, t][:], wave[b, t][:], ACT.Sin, scale=TURN)

        skip_gain = keep.tile([P, PACK], F32, name="skip_gain")
        nc.vector.tensor_tensor(skip_gain[:], skip_sb[:, 0, :], gain_sb[:, 0, :], ALU.mult)

        picked = [late.tile([P, PACK, PICKS], F32, name=f"picked{b}") for b in range(H_PASSES)]
        x_bf16 = [late.tile([P, PICKS, PACK], BF16, name=f"x_bf16{b}", align_bytes=64) for b in range(H_PASSES)]
        x_codes = [late.tile([P, PICKS], U32, name=f"x_codes{b}", align_bytes=64) for b in range(H_PASSES)]
        x_plane = [late.tile([P, PICKS], U8, name=f"x_plane{b}", align_bytes=64) for b in range(H_PASSES)]
        pick_halves = [slice(0, PICKS // 2), slice(PICKS // 2, PICKS)]

        def add_terms(b, t):
            if b == 0:
                nc.vector.tensor_tensor(tone[b, t][:], wave[b, t][:], offset[b, t], ALU.add)
            else:
                nc.vector.scalar_tensor_tensor(
                    tone[b, t][:], wave[b, t][:], gain_sb[:, b, t : t + 1], offset[b, t], ALU.mult, ALU.add
                )

        def quantize_x(b, cols):
            nc.vector.quantize_mx(
                x_codes[b][:, cols].bitcast(FP8X4),
                x_plane[b][:, cols],
                x_bf16[b][:, cols, :].rearrange("p m t -> p (m t)"),
            )

        add_terms(*row_tiles[0])
        for i, (b, t) in enumerate(row_tiles):
            if i + 1 < len(row_tiles):
                add_terms(*row_tiles[i + 1])
            nc.vector.tensor_copy(picked[b][:, t, :], tone[b, t][:].indirect(blur_list[:]))
            if (b, t) == (0, PACK - 1):
                rounded = late.tile([P, PACK, PICKS], BF16, name="rounded")
                for u in range(PACK):
                    nc.scalar.activation(rounded[:, u, :], picked[0][:, u, :], ACT.Copy, scale=gain_sb[:, 0, u : u + 1])
                nc.scalar.copy(x_bf16[0][:], rounded[:].rearrange("p t m -> p m t"))
                quantize_x(0, slice(0, PICKS))
        for cols in pick_halves:
            nc.vector.tensor_copy(x_bf16[1][:, cols, :], picked[1][:, :, cols].rearrange("p t m -> p m t"))
            quantize_x(1, cols)

        for i, (b, t) in enumerate(row_tiles):
            page = keep.tile([P, S], F32, name="wave", bufs=len(row_tiles))
            factor = skip_gain[:, t : t + 1] if b == 0 else skip_sb[:, b, t : t + 1]
            nc.scalar.activation(page[:], tone[b, t][:], ACT.Copy, scale=factor)
            for cols in pick_halves if i == 0 else [slice(0, PICKS)]:
                width = cols.stop - cols.start
                y = psum.tile([P, BANK], F32, name="bank")
                for a in range(H_PASSES):
                    nc.tensor.matmul_mx(
                        y[:, :width],
                        lhsT=w4_codes[:, a, b, t].rearrange("p m e -> p (m e)").bitcast(FP4X4),
                        lhsT_scale=w4_plane[:, a, b, t, :],
                        rhs=x_codes[a][:, cols].bitcast(FP8X4),
                        rhs_scale=x_plane[a][:, cols],
                        start=(a == 0),
                        stop=(a == H_PASSES - 1),
                    )
                mapped = late.tile([P, PICKS], F32, name="mapped", bufs=2)
                nc.scalar.activation(mapped[:, :width], y[:, :width], ACT.Tanh)
                entries = blur_list[:, cols.start // LIST_ROWS : cols.stop // LIST_ROWS]
                nc.vector.tensor_tensor(page[:].indirect(entries), mapped[:, :width], wgo_sb[:, t, cols], ALU.mult)
            nc.sync.dma_start(out_rows[b, t], page[:])
